import numpy as np
import ml_dtypes


def mxq(x, axis, fmt="e4m3"):
    dtype, down = {"e4m3": (ml_dtypes.float8_e4m3fn, 7), "e5m2": (ml_dtypes.float8_e5m2, 14)}[fmt]
    v = np.moveaxis(np.asarray(x, np.float32).astype(ml_dtypes.bfloat16).astype(np.float64), axis, -1)
    blocks = v.reshape(v.shape[:-1] + (-1, 32))
    amax = np.abs(blocks).max(-1, keepdims=True)
    byte = np.maximum(np.where(amax > 0, np.frexp(amax)[1] - 1 + 127, 0) - down, 1)
    scale = np.exp2(byte - 127.0)
    codes = (blocks / scale).astype(np.float32).astype(dtype).astype(np.float64)
    return np.moveaxis((codes * scale).reshape(v.shape), -1, axis)


WIDE = False


def mx_kscale(k):
    if not WIDE:
        return np.ones(k)
    levels = np.array([10, -10, 5, -5, 0])
    if k % 512:
        return np.exp2(np.random.permutation(np.resize(levels, k // 32))).repeat(32)
    a = np.empty((k // 512, 16))
    for p in range(k // 512):
        a[p, :8] = np.random.permutation(np.resize(levels, 8))
        for g in range(8):
            far = levels[np.abs(levels - a[p, g]) >= 10]
            a[p, g + 8] = far[np.random.randint(len(far))]
    return np.exp2(a.ravel()).repeat(32)


def f64(x):
    return np.asarray(x).astype(np.float64)


def striped(idx):
    return np.tile(idx.reshape(-1, 16).T, (8, 1)).astype(np.uint16)


def unstriped(offs):
    return offs[:16].T.reshape(-1).astype(np.int64)


def pack_weight(w):
    k, n = w.shape
    w = f64(np.asarray(w, np.float32).astype(ml_dtypes.bfloat16)).reshape(k // 32, 32, n)
    amax = np.abs(w).max(1)
    byte = np.clip(np.where(amax > 0, np.frexp(amax)[1] - 1 + 127 - 7, 1), 1, 254)
    scaled = (w * np.exp2(127.0 - byte)[:, None, :]).reshape(k, n).astype(np.float32)
    words = np.ascontiguousarray(scaled.reshape(k // 512, 128, 4, n).transpose(0, 1, 3, 2)).astype(ml_dtypes.float8_e4m3fn).view(np.uint8)
    return words, np.ascontiguousarray(byte.astype(np.uint8).reshape(k // 512, 16, n))


def unpack_weight(words, scales):
    g, p, n, _ = words.shape
    vals = np.ascontiguousarray(words).view(ml_dtypes.float8_e4m3fn).astype(np.float64) * np.repeat(np.exp2(scales.astype(np.float64) - 127.0), 8, axis=1)[..., None]
    return vals.transpose(0, 1, 3, 2).reshape(g * 512, n)


K, T, D, S, V, N = 1536, 1024, 3, 512, 256, 128


def setup_inputs():
    n = np.random.standard_normal
    s = mx_kscale(K)[:, None]
    words, scales = pack_weight(n((K, N)) / np.sqrt(K) / s)
    return {
        "xT": (n((K, T)) * s).astype(np.float32),
        "w_words": words,
        "w_scales": scales,
        "gate": np.tile(np.random.uniform(0.2, 1.0, (D, 1, V)) / np.sqrt(D), (1, N, 1)).astype(np.float32),
        "offs": striped(np.random.permutation(T)[:S]),
        "pos1": striped(np.random.permutation(S)[:V]),
        "pos2": striped(np.random.permutation(S)[:V]),
        "pos3": striped(np.random.permutation(S)[:V]),
    }


def reference(xT, w_words, w_scales, gate, offs, pos1, pos2, pos3):
    w = unpack_weight(w_words, w_scales)
    idx = unstriped(offs)
    xq = mxq(f64(xT)[:, idx], 0, "e4m3")
    y = w.T @ xq
    return sum(f64(gate[d]) * y[:, unstriped(p)] for d, p in enumerate((pos1, pos2, pos3)))

@@ -1,0 +1,137 @@
+from contextlib import ExitStack
+
+import concourse.mybir as mybir
+
+K, T, D, S, V, N = 1536, 1024, 3, 512, 256, 128
+
+F32 = mybir.dt.float32
+BF16 = mybir.dt.bfloat16
+I32 = mybir.dt.int32
+U32 = mybir.dt.uint32
+U16 = mybir.dt.uint16
+U8 = mybir.dt.uint8
+FP8X4 = mybir.dt.float8_e4m3fn_x4
+ADD = mybir.AluOpType.add
+MULT = mybir.AluOpType.mult
+
+FLOPS = 2 * K * S * N + 5 * V * N
+
+P = 128
+PACK = 4
+K_PASS = P * PACK
+PASSES = K // K_PASS
+
+CHUNKS = {
+    (0, 0): ((0, 320, 384, 384), (384, 864, 1024, 1024)),
+    (0, 1): ((0, 832, 1024, 1024),),
+    (1, 0): ((0, 832, 1024, 1024),),
+    (1, 1): ((0, 736, 1024, 1024),),
+    (2, 0): ((0, 352, 512, 512), (512, 864, 1024, 1024)),
+    (2, 1): ((0, 352, 512, 512), (512, 656, 656, 768), (768, 896, 896, 1024)),
+}
+PARTS = ((0, 256), (256, 384), (384, 512))
+
+
+def tile_picked_sub_lin_none_sub_e_kernel(
+    tc, xT, w_words, w_scales, gate, offs, pos1, pos2, pos3, out
+):
+    nc = tc.nc
+    with ExitStack() as ctx:
+        held = ctx.enter_context(tc.tile_pool(name="held", bufs=1))
+        psum = ctx.enter_context(tc.psum_pool(name="psum", bufs=1))
+
+        lists = [held.tile([P, src.shape[1]], U16, name=f"list{i}") for i, src in enumerate((offs, pos1, pos2, pos3))]
+        w_codes = held.tile([P, PASSES, N], U32, align_bytes=64, name="w_codes")
+        w_planes = held.tile([P, PASSES, N], U8, align_bytes=64, name="w_planes")
+        gates = held.tile([P, D, V], F32, name="gates")
+
+        nc.gpsimd.memset(w_planes[:].rearrange("p a m -> p (a m)").bitcast(I32), 0)
+
+        raw = {}
+        for a, u in CHUNKS:
+            rows = xT[a * K_PASS : (a + 1) * K_PASS, :].rearrange("(p j) t -> p j t", j=PACK)
+            for chunk in CHUNKS[a, u]:
+                t0, t1 = chunk[0], chunk[-1]
+                tile = held.tile([P, 2, t1 - t0], F32, name=f"raw_{a}_{u}_{t0}")
+                nc.sync.dma_start(out=tile[:], in_=rows[:, 2 * u : 2 * u + 2, t0:t1])
+                raw[a, u, t0] = tile
+            if (a, u) == (0, 0):
+                nc.sync.dma_start(out=lists[0][:], in_=offs)
+        nc.sync.dma_start(
+            out=w_codes[:].bitcast(I32), in_=w_words.rearrange("a p m r -> p a (m r)").bitcast(I32)
+        )
+        for q in range(4):
+            nc.sync.dma_start(
+                out=w_planes[32 * q : 32 * q + 4, :, :].bitcast(I32),
+                in_=w_scales[:, 4 * q : 4 * q + 4, :].rearrange("a q m -> q a m").bitcast(I32),
+            )
+        nc.sync.dma_start(out=gates[:], in_=gate.rearrange("d m v -> m d v"))
+        for i, src in enumerate((pos1, pos2, pos3)):
+            nc.sync.dma_start(out=lists[1 + i][:], in_=src)
+
+        banks = [psum.tile([N, s1 - s0], F32, name=f"bank_{s0}") for s0, s1 in PARTS]
+        y = held.tile([N, S], F32, name="y")
+
+        def cast(a, u, pairs):
+            for chunk in CHUNKS[a, u]:
+                t0 = chunk[0]
+                src = raw[a, u, t0][:].rearrange("p e t -> p t e")
+                for engine, b0, b1 in zip(("scalar", "gpsimd", "vector"), chunk, chunk[1:]):
+                    dst, part = pairs[:, b0:b1, :], src[:, b0 - t0 : b1 - t0, :]
+                    if b1 > b0 and engine == "scalar":
+                        nc.scalar.copy(out=dst, in_=part)
+                    elif b1 > b0 and engine == "gpsimd":
+                        nc.gpsimd.tensor_scalar(out=dst, in0=part, scalar1=1.0, scalar2=0.0, op0=MULT, op1=ADD)
+                    elif b1 > b0:
+                        nc.vector.tensor_copy(out=dst, in_=part)
+
+        def product(a, codes, planes, part):
+            s0, s1 = PARTS[part]
+            nc.tensor.matmul_mx(
+                out=banks[part][:],
+                lhsT=w_codes[:, a, :].bitcast(FP8X4),
+                lhsT_scale=w_planes[:, a, :],
+                rhs=codes[:, s0:s1].bitcast(FP8X4),
+                rhs_scale=planes[:, s0:s1],
+                start=(a == 0),
+                stop=(a == PASSES - 1),
+            )
+
+        for a in range(PASSES):
+            last = a == PASSES - 1
+            picked = held.tile([P, S, PACK], BF16, align_bytes=64, name=f"picked{a}")
+            codes = held.tile([P, S], U32, align_bytes=64, name=f"codes{a}")
+            planes = held.tile([P, S], U8, align_bytes=64, name=f"planes{a}")
+            flat = picked[:].rearrange("p s j -> p (s j)")
+            words = flat.bitcast(U32).rearrange("p (s u) -> p s u", u=2)
+            for u in range(2):
+                pairs = held.tile([P, T, 2], BF16, align_bytes=64, name=f"pairs_{a}_{u}")
+                cast(a, u, pairs)
+                window = pairs[:].rearrange("p t e -> p (t e)").bitcast(U32)
+                for s0, s1 in ((0, 256), (256, 512)) if last and u == 1 else ((0, S),):
+                    nc.vector.tensor_copy(
+                        out=words[:, s0:s1, u], in_=window.indirect(lists[0][:, s0 // 16 : s1 // 16])
+                    )
+            for s0, s1 in PARTS if last else ((0, S),):
+                nc.vector.quantize_mx(
+                    out=codes[:, s0:s1].bitcast(FP8X4),
+                    scales=planes[:, s0:s1],
+                    in_=flat[:, PACK * s0 : PACK * s1],
+                )
+            for part in range(len(PARTS)):
+                product(a, codes, planes, part)
+
+        nc.scalar.copy(out=y[:, 0:256], in_=banks[0][:])
+        nc.vector.tensor_copy(out=y[:, 256:384], in_=banks[1][:])
+        nc.scalar.copy(out=y[:, 384:512], in_=banks[2][:])
+
+        terms = []
+        for d in range(D):
+            term = held.tile([N, V], F32, name=f"term{d}")
+            nc.vector.tensor_tensor(out=term[:], in0=y[:].indirect(lists[1 + d][:]), in1=gates[:, d, :], op=MULT)
+            terms.append(term)
+        first = held.tile([N, V], F32, name="first")
+        total = held.tile([N, V], F32, name="total")
+        nc.vector.tensor_tensor(out=first[:], in0=terms[0][:], in1=terms[1][:], op=ADD)
+        nc.vector.tensor_tensor(out=total[:], in0=first[:], in1=terms[2][:], op=ADD)
+        nc.sync.dma_start(out=out, in_=total[:])

@@ -13,6 +13,7 @@ U8 = mybir.dt.uint8
 FP8X4 = mybir.dt.float8_e4m3fn_x4
 ADD = mybir.AluOpType.add
 MULT = mybir.AluOpType.mult
+COPY = mybir.ActivationFunctionType.Copy
 
 FLOPS = 2 * K * S * N + 5 * V * N
 
@@ -21,14 +22,17 @@ PACK = 4
 K_PASS = P * PACK
 PASSES = K // K_PASS
 
-CHUNKS = {
-    (0, 0): ((0, 320, 384, 384), (384, 864, 1024, 1024)),
-    (0, 1): ((0, 832, 1024, 1024),),
-    (1, 0): ((0, 832, 1024, 1024),),
-    (1, 1): ((0, 736, 1024, 1024),),
-    (2, 0): ((0, 352, 512, 512), (512, 864, 1024, 1024)),
-    (2, 1): ((0, 352, 512, 512), (512, 656, 656, 768), (768, 896, 896, 1024)),
-}
+LOADS = (
+    ((0, 512), (512, 1024)),
+    ((0, 512), (512, 768), (768, 1024)),
+    ((0, 512), (512, 768), (768, 896), (896, 1024)),
+)
+BLOCKS = (
+    ((0, 384, 512), (512, 512, 768), (768, 1024, 1024)),
+    ((0, 320, 512), (512, 768, 768), (768, 768, 1024)),
+    ((0, 0, 256), (256, 512, 512), (512, 640, 768), (768, 896, 896), (896, 896, 1024)),
+)
+ROW = (4, 8, 0)
 PARTS = ((0, 256), (256, 384), (384, 512))
 
 
@@ -44,86 +48,93 @@ def tile_picked_sub_lin_none_sub_e_kernel(
         w_codes = held.tile([P, PASSES, N], U32, align_bytes=64, name="w_codes")
         w_planes = held.tile([P, PASSES, N], U8, align_bytes=64, name="w_planes")
         gates = held.tile([P, D, V], F32, name="gates")
+        all_planes = held.tile([P, T], U8, align_bytes=64, name="all_planes")
 
-        nc.gpsimd.memset(w_planes[:].rearrange("p a m -> p (a m)").bitcast(I32), 0)
+        nc.vector.memset(w_planes[:].rearrange("p a m -> p (a m)").bitcast(I32), 0)
+        nc.vector.memset(all_planes[:].bitcast(I32), 0)
 
         raw = {}
-        for a, u in CHUNKS:
+        for a in range(PASSES):
             rows = xT[a * K_PASS : (a + 1) * K_PASS, :].rearrange("(p j) t -> p j t", j=PACK)
-            for chunk in CHUNKS[a, u]:
-                t0, t1 = chunk[0], chunk[-1]
-                tile = held.tile([P, 2, t1 - t0], F32, name=f"raw_{a}_{u}_{t0}")
-                nc.sync.dma_start(out=tile[:], in_=rows[:, 2 * u : 2 * u + 2, t0:t1])
-                raw[a, u, t0] = tile
-            if (a, u) == (0, 0):
-                nc.sync.dma_start(out=lists[0][:], in_=offs)
+            for t0, t1 in LOADS[a]:
+                tile = held.tile([P, PACK, t1 - t0], F32, name=f"raw_{a}_{t0}")
+                nc.sync.dma_start(out=tile[:], in_=rows[:, :, t0:t1])
+                raw[a, t0] = tile
+            if a == 0:
+                for tile, src in zip(lists, (offs, pos1, pos2, pos3)):
+                    nc.sync.dma_start(out=tile[:], in_=src)
+            if a == 1:
+                for q in range(4):
+                    nc.sync.dma_start(
+                        out=w_planes[32 * q : 32 * q + 4, :, :].bitcast(I32),
+                        in_=w_scales[:, 4 * q : 4 * q + 4, :].rearrange("a q m -> q a m").bitcast(I32),
+                    )
         nc.sync.dma_start(
             out=w_codes[:].bitcast(I32), in_=w_words.rearrange("a p m r -> p a (m r)").bitcast(I32)
         )
-        for q in range(4):
-            nc.sync.dma_start(
-                out=w_planes[32 * q : 32 * q + 4, :, :].bitcast(I32),
-                in_=w_scales[:, 4 * q : 4 * q + 4, :].rearrange("a q m -> q a m").bitcast(I32),
-            )
         nc.sync.dma_start(out=gates[:], in_=gate.rearrange("d m v -> m d v"))
-        for i, src in enumerate((pos1, pos2, pos3)):
-            nc.sync.dma_start(out=lists[1 + i][:], in_=src)
 
         banks = [psum.tile([N, s1 - s0], F32, name=f"bank_{s0}") for s0, s1 in PARTS]
         y = held.tile([N, S], F32, name="y")
+        planes = held.tile([P, S], U8, align_bytes=64, name="planes")
 
-        def cast(a, u, pairs):
-            for chunk in CHUNKS[a, u]:
-                t0 = chunk[0]
-                src = raw[a, u, t0][:].rearrange("p e t -> p t e")
-                for engine, b0, b1 in zip(("scalar", "gpsimd", "vector"), chunk, chunk[1:]):
-                    dst, part = pairs[:, b0:b1, :], src[:, b0 - t0 : b1 - t0, :]
-                    if b1 > b0 and engine == "scalar":
-                        nc.scalar.copy(out=dst, in_=part)
-                    elif b1 > b0 and engine == "gpsimd":
-                        nc.gpsimd.tensor_scalar(out=dst, in0=part, scalar1=1.0, scalar2=0.0, op0=MULT, op1=ADD)
-                    elif b1 > b0:
-                        nc.vector.tensor_copy(out=dst, in_=part)
+        all_codes = [held.tile([P, T], U32, align_bytes=64, name=f"all_codes{a}") for a in range(PASSES)]
+        picked = [held.tile([P, S], U32, align_bytes=64, name=f"picked{a}") for a in range(PASSES)]
+        steps = [(a, block) for a in range(PASSES) for block in BLOCKS[a]]
+        grouped = {}
 
-        def product(a, codes, planes, part):
+        def round_block(a, block):
+            b0, b1, b2 = block
+            t0 = max(first for first, end in LOADS[a] if first <= b0)
+            tile = held.tile([P, (b2 - b0) * PACK], BF16, align_bytes=64, name=f"grouped_{a}_{b0}")
+            grouped[a, b0] = tile
+            for engine, c0, c1 in (("scalar", b0, b1), ("vector", b1, b2)):
+                if c1 > c0:
+                    dst = tile[:, PACK * (c0 - b0) : PACK * (c1 - b0)].rearrange("p (c i j) -> p c j i", i=4, j=PACK)
+                    src = raw[a, t0][:, :, c0 - t0 : c1 - t0].rearrange("p j (c i) -> p c j i", i=4)
+                    if engine == "scalar":
+                        nc.scalar.activation(out=dst, in_=src, func=COPY)
+                    else:
+                        nc.vector.tensor_copy(out=dst, in_=src)
+
+        def pick(dst, table, s0, s1):
+            nc.vector.tensor_copy(out=dst[:, s0:s1], in_=table[:].indirect(lists[0][:, s0 // 16 : s1 // 16]))
+
+        def product(a, part):
             s0, s1 = PARTS[part]
             nc.tensor.matmul_mx(
                 out=banks[part][:],
                 lhsT=w_codes[:, a, :].bitcast(FP8X4),
                 lhsT_scale=w_planes[:, a, :],
-                rhs=codes[:, s0:s1].bitcast(FP8X4),
-                rhs_scale=planes[:, s0:s1],
+                rhs=picked[a][:, s0:s1].bitcast(FP8X4),
+                rhs_scale=planes[ROW[a] :, s0:s1],
                 start=(a == 0),
                 stop=(a == PASSES - 1),
             )
 
-        for a in range(PASSES):
-            last = a == PASSES - 1
-            picked = held.tile([P, S, PACK], BF16, align_bytes=64, name=f"picked{a}")
-            codes = held.tile([P, S], U32, align_bytes=64, name=f"codes{a}")
-            planes = held.tile([P, S], U8, align_bytes=64, name=f"planes{a}")
-            flat = picked[:].rearrange("p s j -> p (s j)")
-            words = flat.bitcast(U32).rearrange("p (s u) -> p s u", u=2)
-            for u in range(2):
-                pairs = held.tile([P, T, 2], BF16, align_bytes=64, name=f"pairs_{a}_{u}")
-                cast(a, u, pairs)
-                window = pairs[:].rearrange("p t e -> p (t e)").bitcast(U32)
-                for s0, s1 in ((0, 256), (256, 512)) if last and u == 1 else ((0, S),):
-                    nc.vector.tensor_copy(
-                        out=words[:, s0:s1, u], in_=window.indirect(lists[0][:, s0 // 16 : s1 // 16])
-                    )
-            for s0, s1 in PARTS if last else ((0, S),):
-                nc.vector.quantize_mx(
-                    out=codes[:, s0:s1].bitcast(FP8X4),
-                    scales=planes[:, s0:s1],
-                    in_=flat[:, PACK * s0 : PACK * s1],
-                )
-            for part in range(len(PARTS)):
-                product(a, codes, planes, part)
+        round_block(*steps[0])
+        for i, (a, block) in enumerate(steps):
+            if i + 1 < len(steps):
+                round_block(*steps[i + 1])
+            if block[0] == 0 and a > 0:
+                pick(picked[a - 1], all_codes[a - 1], 0, S)
+            nc.vector.quantize_mx(
+                out=all_codes[a][:, block[0] : block[2]].bitcast(FP8X4),
+                scales=all_planes[ROW[a] :, block[0] : block[2]],
+                in_=grouped[a, block[0]][:],
+            )
 
-        nc.scalar.copy(out=y[:, 0:256], in_=banks[0][:])
-        nc.vector.tensor_copy(out=y[:, 256:384], in_=banks[1][:])
-        nc.scalar.copy(out=y[:, 384:512], in_=banks[2][:])
+        for parts in ((0,), (1, 2)):
+            pick(planes, all_planes, PARTS[parts[0]][0], PARTS[parts[-1]][1])
+            for part in parts:
+                pick(picked[-1], all_codes[-1], *PARTS[part])
+            for a in range(PASSES):
+                for part in parts:
+                    product(a, part)
+
+        for bank, (s0, s1) in zip(banks[:-1], PARTS):
+            nc.scalar.copy(out=y[:, s0:s1], in_=bank[:])
+        nc.vector.tensor_copy(out=y[:, PARTS[-1][0] :], in_=banks[-1][:])
 
         terms = []
         for d in range(D):

@@ -61,17 +61,17 @@ def tile_picked_sub_lin_none_sub_e_kernel(
                 nc.sync.dma_start(out=tile[:], in_=rows[:, :, t0:t1])
                 raw[a, t0] = tile
             if a == 0:
-                for tile, src in zip(lists, (offs, pos1, pos2, pos3)):
-                    nc.sync.dma_start(out=tile[:], in_=src)
-            if a == 1:
-                for q in range(4):
-                    nc.sync.dma_start(
-                        out=w_planes[32 * q : 32 * q + 4, :, :].bitcast(I32),
-                        in_=w_scales[:, 4 * q : 4 * q + 4, :].rearrange("a q m -> q a m").bitcast(I32),
-                    )
+                nc.sync.dma_start(out=lists[0][:], in_=offs)
         nc.sync.dma_start(
             out=w_codes[:].bitcast(I32), in_=w_words.rearrange("a p m r -> p a (m r)").bitcast(I32)
         )
+        for q in range(4):
+            nc.sync.dma_start(
+                out=w_planes[32 * q : 32 * q + 4, :, :].bitcast(I32),
+                in_=w_scales[:, 4 * q : 4 * q + 4, :].rearrange("a q m -> q a m").bitcast(I32),
+            )
+        for tile, src in zip(lists[1:], (pos1, pos2, pos3)):
+            nc.sync.dma_start(out=tile[:], in_=src)
         nc.sync.dma_start(out=gates[:], in_=gate.rearrange("d m v -> m d v"))
 
         banks = [psum.tile([N, s1 - s0], F32, name=f"bank_{s0}") for s0, s1 in PARTS]
@@ -136,13 +136,24 @@ def tile_picked_sub_lin_none_sub_e_kernel(
             nc.scalar.copy(out=y[:, s0:s1], in_=bank[:])
         nc.vector.tensor_copy(out=y[:, PARTS[-1][0] :], in_=banks[-1][:])
 
-        terms = []
-        for d in range(D):
-            term = held.tile([N, V], F32, name=f"term{d}")
-            nc.vector.tensor_tensor(out=term[:], in0=y[:].indirect(lists[1 + d][:]), in1=gates[:, d, :], op=MULT)
-            terms.append(term)
+        terms = [held.tile([N, V], F32, name=f"term{d}") for d in range(D)]
         first = held.tile([N, V], F32, name="first")
         total = held.tile([N, V], F32, name="total")
+        halves = ((0, V // 2), (V // 2, V))
+
+        def fetch(d, v0, v1):
+            nc.vector.tensor_tensor(
+                out=terms[d][:, v0:v1],
+                in0=y[:].indirect(lists[1 + d][:, v0 // 16 : v1 // 16]),
+                in1=gates[:, d, v0:v1],
+                op=MULT,
+            )
+
+        fetch(0, 0, V)
+        fetch(1, 0, V)
+        fetch(2, *halves[0])
         nc.vector.tensor_tensor(out=first[:], in0=terms[0][:], in1=terms[1][:], op=ADD)
-        nc.vector.tensor_tensor(out=total[:], in0=first[:], in1=terms[2][:], op=ADD)
-        nc.sync.dma_start(out=out, in_=total[:])
+        fetch(2, *halves[1])
+        for queue, (v0, v1) in zip((nc.sync, nc.scalar), halves):
+            nc.vector.tensor_tensor(out=total[:, v0:v1], in0=first[:, v0:v1], in1=terms[2][:, v0:v1], op=ADD)
+            queue.dma_start(out=out[:, v0:v1], in_=total[:, v0:v1])

@@ -24,16 +24,16 @@ PASSES = K // K_PASS
 
 LOADS = (
     ((0, 512), (512, 1024)),
-    ((0, 512), (512, 768), (768, 1024)),
-    ((0, 512), (512, 768), (768, 896), (896, 1024)),
+    ((0, 256), (256, 512), (512, 768), (768, 1024)),
+    ((0, 256), (256, 512), (512, 768), (768, 896), (896, 1024)),
 )
 BLOCKS = (
-    ((0, 384, 512), (512, 512, 768), (768, 1024, 1024)),
-    ((0, 320, 512), (512, 768, 768), (768, 768, 1024)),
-    ((0, 0, 256), (256, 512, 512), (512, 640, 768), (768, 896, 896), (896, 896, 1024)),
+    ((0, 0, 256), (256, 512, 512), (512, 512, 768), (768, 1024, 1024)),
+    ((0, 256, 256), (256, 512, 512), (512, 512, 768), (768, 896, 1024)),
+    ((0, 256, 256), (256, 384, 512), (512, 640, 768), (768, 896, 896), (896, 928, 1024)),
 )
 ROW = (4, 8, 0)
-PARTS = ((0, 256), (256, 384), (384, 512))
+PARTS = ((0, 128), (128, 384), (384, 512))
 
 
 def tile_picked_sub_lin_none_sub_e_kernel(
@@ -124,13 +124,15 @@ def tile_picked_sub_lin_none_sub_e_kernel(
                 in_=grouped[a, block[0]][:],
             )
 
-        for parts in ((0,), (1, 2)):
-            pick(planes, all_planes, PARTS[parts[0]][0], PARTS[parts[-1]][1])
-            for part in parts:
-                pick(picked[-1], all_codes[-1], *PARTS[part])
-            for a in range(PASSES):
-                for part in parts:
-                    product(a, part)
+        for s0, s1 in PARTS:
+            pick(planes, all_planes, s0, s1)
+        for part in (1, 0, 2):
+            pick(picked[-1], all_codes[-1], *PARTS[part])
+        for part in range(len(PARTS)):
+            for a in range(PASSES - 1):
+                product(a, part)
+        for part in (1, 0, 2):
+            product(PASSES - 1, part)
 
         for bank, (s0, s1) in zip(banks[:-1], PARTS):
             nc.scalar.copy(out=y[:, s0:s1], in_=bank[:])

@@ -30,7 +30,7 @@ LOADS = (
 BLOCKS = (
     ((0, 0, 256), (256, 512, 512), (512, 512, 768), (768, 1024, 1024)),
     ((0, 256, 256), (256, 512, 512), (512, 512, 768), (768, 896, 1024)),
-    ((0, 256, 256), (256, 384, 512), (512, 640, 768), (768, 896, 896), (896, 928, 1024)),
+    ((0, 256, 256), (256, 512, 512), (512, 576, 768), (768, 896, 896), (896, 896, 1024)),
 )
 ROW = (4, 8, 0)
 PARTS = ((0, 128), (128, 384), (384, 512))
@@ -70,9 +70,9 @@ def tile_picked_sub_lin_none_sub_e_kernel(
                 out=w_planes[32 * q : 32 * q + 4, :, :].bitcast(I32),
                 in_=w_scales[:, 4 * q : 4 * q + 4, :].rearrange("a q m -> q a m").bitcast(I32),
             )
+        nc.sync.dma_start(out=gates[:], in_=gate.rearrange("d m v -> m d v"))
         for tile, src in zip(lists[1:], (pos1, pos2, pos3)):
             nc.sync.dma_start(out=tile[:], in_=src)
-        nc.sync.dma_start(out=gates[:], in_=gate.rearrange("d m v -> m d v"))
 
         banks = [psum.tile([N, s1 - s0], F32, name=f"bank_{s0}") for s0, s1 in PARTS]
         y = held.tile([N, S], F32, name="y")
@@ -134,9 +134,9 @@ def tile_picked_sub_lin_none_sub_e_kernel(
         for part in (1, 0, 2):
             product(PASSES - 1, part)
 
-        for bank, (s0, s1) in zip(banks[:-1], PARTS):
+        nc.vector.tensor_copy(out=y[:, : PARTS[0][1]], in_=banks[0][:])
+        for bank, (s0, s1) in zip(banks[1:], PARTS[1:]):
             nc.scalar.copy(out=y[:, s0:s1], in_=bank[:])
-        nc.vector.tensor_copy(out=y[:, PARTS[-1][0] :], in_=banks[-1][:])
 
         terms = [held.tile([N, V], F32, name=f"term{d}") for d in range(D)]
         first = held.tile([N, V], F32, name="first")

@@ -33,7 +33,7 @@ BLOCKS = (
     ((0, 256, 256), (256, 512, 512), (512, 576, 768), (768, 896, 896), (896, 896, 1024)),
 )
 ROW = (4, 8, 0)
-PARTS = ((0, 128), (128, 384), (384, 512))
+PARTS = ((0, 256), (256, 384), (384, 512))
 
 
 def tile_picked_sub_lin_none_sub_e_kernel(
@@ -124,22 +124,22 @@ def tile_picked_sub_lin_none_sub_e_kernel(
                 in_=grouped[a, block[0]][:],
             )
 
+        pick(planes, all_planes, 0, S // 2)
+        pick(planes, all_planes, S // 2, S)
         for s0, s1 in PARTS:
-            pick(planes, all_planes, s0, s1)
-        for part in (1, 0, 2):
-            pick(picked[-1], all_codes[-1], *PARTS[part])
+            pick(picked[-1], all_codes[-1], s0, s1)
         for part in range(len(PARTS)):
             for a in range(PASSES - 1):
                 product(a, part)
-        for part in (1, 0, 2):
+        for part in range(len(PARTS)):
             product(PASSES - 1, part)
 
-        nc.vector.tensor_copy(out=y[:, : PARTS[0][1]], in_=banks[0][:])
-        for bank, (s0, s1) in zip(banks[1:], PARTS[1:]):
-            nc.scalar.copy(out=y[:, s0:s1], in_=bank[:])
+        nc.scalar.copy(out=y[:, slice(*PARTS[0])], in_=banks[0][:])
+        nc.vector.tensor_copy(out=y[:, slice(*PARTS[1])], in_=banks[1][:])
+        nc.scalar.copy(out=y[:, slice(*PARTS[2])], in_=banks[2][:])
 
         terms = [held.tile([N, V], F32, name=f"term{d}") for d in range(D)]
-        first = held.tile([N, V], F32, name="first")
+        first = gates[:].rearrange("p d v -> p (d v)")[:, V + V // 2 : 2 * V + V // 2]
         total = held.tile([N, V], F32, name="total")
         halves = ((0, V // 2), (V // 2, V))
 
@@ -154,8 +154,8 @@ def tile_picked_sub_lin_none_sub_e_kernel(
         fetch(0, 0, V)
         fetch(1, 0, V)
         fetch(2, *halves[0])
-        nc.vector.tensor_tensor(out=first[:], in0=terms[0][:], in1=terms[1][:], op=ADD)
+        nc.vector.tensor_tensor(out=first, in0=terms[0][:], in1=terms[1][:], op=ADD)
         fetch(2, *halves[1])
-        for queue, (v0, v1) in zip((nc.sync, nc.scalar), halves):
+        for queue, (v0, v1) in zip((nc.scalar, nc.sync), halves):
             nc.vector.tensor_tensor(out=total[:, v0:v1], in0=first[:, v0:v1], in1=terms[2][:, v0:v1], op=ADD)
             queue.dma_start(out=out[:, v0:v1], in_=total[:, v0:v1])

@@ -22,17 +22,8 @@ PACK = 4
 K_PASS = P * PACK
 PASSES = K // K_PASS
 
-LOADS = (
-    ((0, 512), (512, 1024)),
-    ((0, 256), (256, 512), (512, 768), (768, 1024)),
-    ((0, 256), (256, 512), (512, 768), (768, 896), (896, 1024)),
-)
-BLOCKS = (
-    ((0, 0, 256), (256, 512, 512), (512, 512, 768), (768, 1024, 1024)),
-    ((0, 256, 256), (256, 512, 512), (512, 512, 768), (768, 896, 1024)),
-    ((0, 256, 256), (256, 512, 512), (512, 576, 768), (768, 896, 896), (896, 896, 1024)),
-)
-ROW = (4, 8, 0)
+VECTOR_SHARE = ((288, 288, 288, 256), (0, 192, 288, 256), (0, 128, 224, 224))
+LAST_CUT = 384
 PARTS = ((0, 256), (256, 384), (384, 512))
 
 
@@ -48,20 +39,18 @@ def tile_picked_sub_lin_none_sub_e_kernel(
         w_codes = held.tile([P, PASSES, N], U32, align_bytes=64, name="w_codes")
         w_planes = held.tile([P, PASSES, N], U8, align_bytes=64, name="w_planes")
         gates = held.tile([P, D, V], F32, name="gates")
-        all_planes = held.tile([P, T], U8, align_bytes=64, name="all_planes")
 
         nc.vector.memset(w_planes[:].rearrange("p a m -> p (a m)").bitcast(I32), 0)
-        nc.vector.memset(all_planes[:].bitcast(I32), 0)
 
         raw = {}
         for a in range(PASSES):
             rows = xT[a * K_PASS : (a + 1) * K_PASS, :].rearrange("(p j) t -> p j t", j=PACK)
-            for t0, t1 in LOADS[a]:
-                tile = held.tile([P, PACK, t1 - t0], F32, name=f"raw_{a}_{t0}")
-                nc.sync.dma_start(out=tile[:], in_=rows[:, :, t0:t1])
-                raw[a, t0] = tile
-            if a == 0:
-                nc.sync.dma_start(out=lists[0][:], in_=offs)
+            for j in range(PACK):
+                tile = held.tile([P, T], F32, name=f"raw_{a}_{j}")
+                nc.sync.dma_start(out=tile[:], in_=rows[:, j, :])
+                raw[a, j] = tile
+                if (a, j) == (0, 0):
+                    nc.sync.dma_start(out=lists[0][:], in_=offs)
         nc.sync.dma_start(
             out=w_codes[:].bitcast(I32), in_=w_words.rearrange("a p m r -> p a (m r)").bitcast(I32)
         )
@@ -76,29 +65,36 @@ def tile_picked_sub_lin_none_sub_e_kernel(
 
         banks = [psum.tile([N, s1 - s0], F32, name=f"bank_{s0}") for s0, s1 in PARTS]
         y = held.tile([N, S], F32, name="y")
-        planes = held.tile([P, S], U8, align_bytes=64, name="planes")
+        picked = [held.tile([P, PACK, S], BF16, name=f"picked{a}") for a in range(PASSES)]
+        grouped = [held.tile([P, S * PACK], BF16, align_bytes=64, name=f"grouped{a}") for a in range(PASSES)]
+        codes = [held.tile([P, S], U32, align_bytes=64, name=f"codes{a}") for a in range(PASSES)]
+        planes = [held.tile([P, S], U8, align_bytes=64, name=f"planes{a}") for a in range(PASSES)]
 
-        all_codes = [held.tile([P, T], U32, align_bytes=64, name=f"all_codes{a}") for a in range(PASSES)]
-        picked = [held.tile([P, S], U32, align_bytes=64, name=f"picked{a}") for a in range(PASSES)]
-        steps = [(a, block) for a in range(PASSES) for block in BLOCKS[a]]
-        grouped = {}
+        def pick(engine, a, j, s0, s1):
+            window = raw[a, j][:].indirect(lists[0][:, s0 // 16 : s1 // 16])
+            if engine == "scalar":
+                nc.scalar.activation(out=picked[a][:, j, s0:s1], in_=window, func=COPY)
+            else:
+                nc.vector.tensor_copy(out=picked[a][:, j, s0:s1], in_=window)
 
-        def round_block(a, block):
-            b0, b1, b2 = block
-            t0 = max(first for first, end in LOADS[a] if first <= b0)
-            tile = held.tile([P, (b2 - b0) * PACK], BF16, align_bytes=64, name=f"grouped_{a}_{b0}")
-            grouped[a, b0] = tile
-            for engine, c0, c1 in (("scalar", b0, b1), ("vector", b1, b2)):
-                if c1 > c0:
-                    dst = tile[:, PACK * (c0 - b0) : PACK * (c1 - b0)].rearrange("p (c i j) -> p c j i", i=4, j=PACK)
-                    src = raw[a, t0][:, :, c0 - t0 : c1 - t0].rearrange("p j (c i) -> p c j i", i=4)
-                    if engine == "scalar":
-                        nc.scalar.activation(out=dst, in_=src, func=COPY)
-                    else:
-                        nc.vector.tensor_copy(out=dst, in_=src)
+        def pick_in_place(a, j, s0, s1):
+            dst = grouped[a][:, PACK * s0 : PACK * s1].rearrange("p (s j) -> p s j", j=PACK)[:, :, j]
+            nc.vector.tensor_copy(out=dst, in_=raw[a, j][:].indirect(lists[0][:, s0 // 16 : s1 // 16]))
 
-        def pick(dst, table, s0, s1):
-            nc.vector.tensor_copy(out=dst[:, s0:s1], in_=table[:].indirect(lists[0][:, s0 // 16 : s1 // 16]))
+        def place(a, j0, j1, s0, s1):
+            dst = grouped[a][:, PACK * s0 : PACK * s1].rearrange("p (s j) -> p s j", j=PACK)[:, :, j0:j1]
+            nc.vector.tensor_copy(out=dst, in_=picked[a][:, j0:j1, s0:s1].rearrange("p j s -> p s j"))
+
+        def weave(a, s0, s1):
+            dst = grouped[a][:, PACK * s0 : PACK * s1].rearrange("p (c i j) -> p c j i", i=4, j=PACK)
+            nc.vector.tensor_copy(out=dst, in_=picked[a][:, :, s0:s1].rearrange("p j (c i) -> p c j i", i=4))
+
+        def quantise(a, s0, s1):
+            nc.vector.quantize_mx(
+                out=codes[a][:, s0:s1].bitcast(FP8X4),
+                scales=planes[a][:, s0:s1],
+                in_=grouped[a][:, PACK * s0 : PACK * s1],
+            )
 
         def product(a, part):
             s0, s1 = PARTS[part]
@@ -106,56 +102,75 @@ def tile_picked_sub_lin_none_sub_e_kernel(
                 out=banks[part][:],
                 lhsT=w_codes[:, a, :].bitcast(FP8X4),
                 lhsT_scale=w_planes[:, a, :],
-                rhs=picked[a][:, s0:s1].bitcast(FP8X4),
-                rhs_scale=planes[ROW[a] :, s0:s1],
+                rhs=codes[a][:, s0:s1].bitcast(FP8X4),
+                rhs_scale=planes[a][:, s0:s1],
                 start=(a == 0),
                 stop=(a == PASSES - 1),
             )
 
-        round_block(*steps[0])
-        for i, (a, block) in enumerate(steps):
-            if i + 1 < len(steps):
-                round_block(*steps[i + 1])
-            if block[0] == 0 and a > 0:
-                pick(picked[a - 1], all_codes[a - 1], 0, S)
-            nc.vector.quantize_mx(
-                out=all_codes[a][:, block[0] : block[2]].bitcast(FP8X4),
-                scales=all_planes[ROW[a] :, block[0] : block[2]],
-                in_=grouped[a, block[0]][:],
-            )
+        last = PASSES - 1
+        half = S // 2
+        in_place = VECTOR_SHARE[last][-1]
+        for a in range(PASSES):
+            for j in range(PACK):
+                share = VECTOR_SHARE[a][j]
+                if a == last and j >= 2:
+                    pick_in_place(a, j, 0, share)
+                elif share:
+                    pick("vector", a, j, 0, share)
+                if (a, j) == (last, 1):
+                    pick("scalar", a, j, share, in_place)
+                    pick("scalar", a, j, in_place, S)
+                    place(a, 0, 2, 0, in_place)
+                elif (a, j) == (last, PACK - 1):
+                    pick("scalar", a, j, share, LAST_CUT)
+                    pick("scalar", a, j, LAST_CUT, S)
+                else:
+                    pick("scalar", a, j, share, S)
+            if a < last:
+                weave(a, 0, half)
+                weave(a, half, S)
+            else:
+                weave(a, in_place, LAST_CUT)
+                weave(a, LAST_CUT, S)
+            for s0 in (0, half):
+                quantise(a, s0, s0 + half)
 
-        pick(planes, all_planes, 0, S // 2)
-        pick(planes, all_planes, S // 2, S)
-        for s0, s1 in PARTS:
-            pick(picked[-1], all_codes[-1], s0, s1)
         for part in range(len(PARTS)):
             for a in range(PASSES - 1):
                 product(a, part)
         for part in range(len(PARTS)):
-            product(PASSES - 1, part)
+            product(last, part)
 
         nc.scalar.copy(out=y[:, slice(*PARTS[0])], in_=banks[0][:])
-        nc.vector.tensor_copy(out=y[:, slice(*PARTS[1])], in_=banks[1][:])
-        nc.scalar.copy(out=y[:, slice(*PARTS[2])], in_=banks[2][:])
+        nc.scalar.copy(out=y[:, slice(*PARTS[1])], in_=banks[1][:])
+        nc.vector.tensor_copy(out=y[:, slice(*PARTS[2])], in_=banks[2][:])
 
         terms = [held.tile([N, V], F32, name=f"term{d}") for d in range(D)]
-        first = gates[:].rearrange("p d v -> p (d v)")[:, V + V // 2 : 2 * V + V // 2]
+        fetched = [held.tile([N, V], F32, name=f"fetched{d}") for d in range(1, D)]
+        first = held.tile([N, V], F32, name="first")
         total = held.tile([N, V], F32, name="total")
-        halves = ((0, V // 2), (V // 2, V))
+        halves = (slice(0, V // 2), slice(V // 2, V))
 
-        def fetch(d, v0, v1):
-            nc.vector.tensor_tensor(
-                out=terms[d][:, v0:v1],
-                in0=y[:].indirect(lists[1 + d][:, v0 // 16 : v1 // 16]),
-                in1=gates[:, d, v0:v1],
-                op=MULT,
-            )
+        def neighbours(d, vs):
+            return y[:].indirect(lists[1 + d][:, vs.start // 16 : vs.stop // 16])
 
-        fetch(0, 0, V)
-        fetch(1, 0, V)
-        fetch(2, *halves[0])
-        nc.vector.tensor_tensor(out=first, in0=terms[0][:], in1=terms[1][:], op=ADD)
-        fetch(2, *halves[1])
-        for queue, (v0, v1) in zip((nc.scalar, nc.sync), halves):
-            nc.vector.tensor_tensor(out=total[:, v0:v1], in0=first[:, v0:v1], in1=terms[2][:, v0:v1], op=ADD)
-            queue.dma_start(out=out[:, v0:v1], in_=total[:, v0:v1])
+        def scale(d, vs):
+            nc.vector.tensor_tensor(out=terms[d][:, vs], in0=fetched[d - 1][:, vs], in1=gates[:, d, vs], op=MULT)
+
+        def add(dst, left, right, vs):
+            nc.vector.tensor_tensor(out=dst[:, vs], in0=left[:, vs], in1=right[:, vs], op=ADD)
+
+        for vs in halves:
+            for d in range(1, D):
+                nc.scalar.activation(out=fetched[d - 1][:, vs], in_=neighbours(d, vs), func=COPY)
+        nc.vector.tensor_tensor(out=terms[0][:], in0=neighbours(0, slice(0, V)), in1=gates[:, 0, :], op=MULT)
+        scale(1, halves[0])
+        scale(2, halves[0])
+        add(first, terms[0], terms[1], halves[0])
+        scale(1, halves[1])
+        scale(2, halves[1])
+        add(first, terms[0], terms[1], halves[1])
+        for queue, vs in zip((nc.scalar, nc.sync), halves):
+            add(total, first, terms[2], vs)
+            queue.dma_start(out=out[:, vs], in_=total[:, vs])

@@ -40,7 +40,13 @@ def tile_picked_sub_lin_none_sub_e_kernel(
         w_planes = held.tile([P, PASSES, N], U8, align_bytes=64, name="w_planes")
         gates = held.tile([P, D, V], F32, name="gates")
 
-        nc.vector.memset(w_planes[:].rearrange("p a m -> p (a m)").bitcast(I32), 0)
+        nc.gpsimd.memset(w_planes[:].rearrange("p a m -> p (a m)").bitcast(I32), 0)
+
+        for q in range(4):
+            nc.scalar.dma_start(
+                out=w_planes[32 * q : 32 * q + 4, :, :].bitcast(I32),
+                in_=w_scales[:, 4 * q : 4 * q + 4, :].rearrange("a q m -> q a m").bitcast(I32),
+            )
 
         raw = {}
         for a in range(PASSES):
@@ -54,11 +60,6 @@ def tile_picked_sub_lin_none_sub_e_kernel(
         nc.sync.dma_start(
             out=w_codes[:].bitcast(I32), in_=w_words.rearrange("a p m r -> p a (m r)").bitcast(I32)
         )
-        for q in range(4):
-            nc.sync.dma_start(
-                out=w_planes[32 * q : 32 * q + 4, :, :].bitcast(I32),
-                in_=w_scales[:, 4 * q : 4 * q + 4, :].rearrange("a q m -> q a m").bitcast(I32),
-            )
         nc.sync.dma_start(out=gates[:], in_=gate.rearrange("d m v -> m d v"))
         for tile, src in zip(lists[1:], (pos1, pos2, pos3)):
             nc.sync.dma_start(out=tile[:], in_=src)

@@ -24,6 +24,7 @@ PASSES = K // K_PASS
 
 VECTOR_SHARE = ((288, 288, 288, 256), (0, 192, 288, 256), (0, 128, 224, 224))
 LAST_CUT = 384
+LOADS = (((0, 2), (2, 4)), ((0, 1), (1, 2), (2, 3), (3, 4)), ((0, 1), (1, 2), (2, 3), (3, 4)))
 PARTS = ((0, 256), (256, 384), (384, 512))
 
 
@@ -51,11 +52,12 @@ def tile_picked_sub_lin_none_sub_e_kernel(
         raw = {}
         for a in range(PASSES):
             rows = xT[a * K_PASS : (a + 1) * K_PASS, :].rearrange("(p j) t -> p j t", j=PACK)
-            for j in range(PACK):
-                tile = held.tile([P, T], F32, name=f"raw_{a}_{j}")
-                nc.sync.dma_start(out=tile[:], in_=rows[:, j, :])
-                raw[a, j] = tile
-                if (a, j) == (0, 0):
+            for j0, j1 in LOADS[a]:
+                tile = held.tile([P, j1 - j0, T], F32, name=f"raw_{a}_{j0}")
+                nc.sync.dma_start(out=tile[:], in_=rows[:, j0:j1, :])
+                for j in range(j0, j1):
+                    raw[a, j] = tile[:, j - j0, :]
+                if (a, j0) == (0, 0):
                     nc.sync.dma_start(out=lists[0][:], in_=offs)
         nc.sync.dma_start(
             out=w_codes[:].bitcast(I32), in_=w_words.rearrange("a p m r -> p a (m r)").bitcast(I32)
@@ -66,13 +68,13 @@ def tile_picked_sub_lin_none_sub_e_kernel(
 
         banks = [psum.tile([N, s1 - s0], F32, name=f"bank_{s0}") for s0, s1 in PARTS]
         y = held.tile([N, S], F32, name="y")
-        picked = [held.tile([P, PACK, S], BF16, name=f"picked{a}") for a in range(PASSES)]
+        picked = [held.tile([P, PACK, S], F32 if a == 0 else BF16, name=f"picked{a}") for a in range(PASSES)]
         grouped = [held.tile([P, S * PACK], BF16, align_bytes=64, name=f"grouped{a}") for a in range(PASSES)]
         codes = [held.tile([P, S], U32, align_bytes=64, name=f"codes{a}") for a in range(PASSES)]
         planes = [held.tile([P, S], U8, align_bytes=64, name=f"planes{a}") for a in range(PASSES)]
 
         def pick(engine, a, j, s0, s1):
-            window = raw[a, j][:].indirect(lists[0][:, s0 // 16 : s1 // 16])
+            window = raw[a, j].indirect(lists[0][:, s0 // 16 : s1 // 16])
             if engine == "scalar":
                 nc.scalar.activation(out=picked[a][:, j, s0:s1], in_=window, func=COPY)
             else:
@@ -80,7 +82,7 @@ def tile_picked_sub_lin_none_sub_e_kernel(
 
         def pick_in_place(a, j, s0, s1):
             dst = grouped[a][:, PACK * s0 : PACK * s1].rearrange("p (s j) -> p s j", j=PACK)[:, :, j]
-            nc.vector.tensor_copy(out=dst, in_=raw[a, j][:].indirect(lists[0][:, s0 // 16 : s1 // 16]))
+            nc.vector.tensor_copy(out=dst, in_=raw[a, j].indirect(lists[0][:, s0 // 16 : s1 // 16]))
 
         def place(a, j0, j1, s0, s1):
             dst = grouped[a][:, PACK * s0 : PACK * s1].rearrange("p (s j) -> p s j", j=PACK)[:, :, j0:j1]
@@ -134,8 +136,8 @@ def tile_picked_sub_lin_none_sub_e_kernel(
             else:
                 weave(a, in_place, LAST_CUT)
                 weave(a, LAST_CUT, S)
-            for s0 in (0, half):
-                quantise(a, s0, s0 + half)
+            for s0, s1 in PARTS if a == last else ((0, half), (half, S)):
+                quantise(a, s0, s1)
 
         for part in range(len(PARTS)):
             for a in range(PASSES - 1):

@@ -49,6 +49,9 @@ def tile_picked_sub_lin_none_sub_e_kernel(
                 in_=w_scales[:, 4 * q : 4 * q + 4, :].rearrange("a q m -> q a m").bitcast(I32),
             )
 
+        warm = held.tile([P, 16], F32, name="warm")
+        nc.vector.memset(warm[:, 0:1], 0.0)
+        nc.scalar.activation(out=warm[:, 8:9], in_=warm[:, 0:1], func=COPY)
         raw = {}
         for a in range(PASSES):
             rows = xT[a * K_PASS : (a + 1) * K_PASS, :].rearrange("(p j) t -> p j t", j=PACK)

@@ -43,12 +43,6 @@ def tile_picked_sub_lin_none_sub_e_kernel(
 
         nc.gpsimd.memset(w_planes[:].rearrange("p a m -> p (a m)").bitcast(I32), 0)
 
-        for q in range(4):
-            nc.scalar.dma_start(
-                out=w_planes[32 * q : 32 * q + 4, :, :].bitcast(I32),
-                in_=w_scales[:, 4 * q : 4 * q + 4, :].rearrange("a q m -> q a m").bitcast(I32),
-            )
-
         warm = held.tile([P, 16], F32, name="warm")
         nc.vector.memset(warm[:, 0:1], 0.0)
         nc.scalar.activation(out=warm[:, 8:9], in_=warm[:, 0:1], func=COPY)
@@ -62,9 +56,14 @@ def tile_picked_sub_lin_none_sub_e_kernel(
                     raw[a, j] = tile[:, j - j0, :]
                 if (a, j0) == (0, 0):
                     nc.sync.dma_start(out=lists[0][:], in_=offs)
-        nc.sync.dma_start(
-            out=w_codes[:].bitcast(I32), in_=w_words.rearrange("a p m r -> p a (m r)").bitcast(I32)
-        )
+        words = w_words.rearrange("a p m r -> p a (m r)").bitcast(I32)
+        nc.sync.dma_start(out=w_codes[:, :1, :].bitcast(I32), in_=words[:, :1, :])
+        for q in range(4):
+            nc.sync.dma_start(
+                out=w_planes[32 * q : 32 * q + 4, :, :].bitcast(I32),
+                in_=w_scales[:, 4 * q : 4 * q + 4, :].rearrange("a q m -> q a m").bitcast(I32),
+            )
+        nc.sync.dma_start(out=w_codes[:, 1:, :].bitcast(I32), in_=words[:, 1:, :])
         nc.sync.dma_start(out=gates[:], in_=gate.rearrange("d m v -> m d v"))
         for tile, src in zip(lists[1:], (pos1, pos2, pos3)):
             nc.sync.dma_start(out=tile[:], in_=src)
@@ -142,11 +141,9 @@ def tile_picked_sub_lin_none_sub_e_kernel(
             for s0, s1 in PARTS if a == last else ((0, half), (half, S)):
                 quantise(a, s0, s1)
 
-        for part in range(len(PARTS)):
-            for a in range(PASSES - 1):
+        for a in range(PASSES):
+            for part in range(len(PARTS)):
                 product(a, part)
-        for part in range(len(PARTS)):
-            product(last, part)
 
         nc.scalar.copy(out=y[:, slice(*PARTS[0])], in_=banks[0][:])
         nc.scalar.copy(out=y[:, slice(*PARTS[1])], in_=banks[1][:])

@@ -24,7 +24,7 @@ PASSES = K // K_PASS
 
 VECTOR_SHARE = ((288, 288, 288, 256), (0, 192, 288, 256), (0, 128, 224, 224))
 LAST_CUT = 384
-LOADS = (((0, 2), (2, 4)), ((0, 1), (1, 2), (2, 3), (3, 4)), ((0, 1), (1, 2), (2, 3), (3, 4)))
+LOADS = (((0, 2), (2, 4)), ((0, 2), (2, 3), (3, 4)), ((0, 1), (1, 2), (2, 3), (3, 4)))
 PARTS = ((0, 256), (256, 384), (384, 512))
 
 
@@ -63,14 +63,15 @@ def tile_picked_sub_lin_none_sub_e_kernel(
                 out=w_planes[32 * q : 32 * q + 4, :, :].bitcast(I32),
                 in_=w_scales[:, 4 * q : 4 * q + 4, :].rearrange("a q m -> q a m").bitcast(I32),
             )
-        nc.sync.dma_start(out=w_codes[:, 1:, :].bitcast(I32), in_=words[:, 1:, :])
+        for a in range(1, PASSES):
+            nc.sync.dma_start(out=w_codes[:, a, :].bitcast(I32), in_=words[:, a, :])
         nc.sync.dma_start(out=gates[:], in_=gate.rearrange("d m v -> m d v"))
         for tile, src in zip(lists[1:], (pos1, pos2, pos3)):
             nc.sync.dma_start(out=tile[:], in_=src)
 
         banks = [psum.tile([N, s1 - s0], F32, name=f"bank_{s0}") for s0, s1 in PARTS]
         y = held.tile([N, S], F32, name="y")
-        picked = [held.tile([P, PACK, S], F32 if a == 0 else BF16, name=f"picked{a}") for a in range(PASSES)]
+        picked = [held.tile([P, PACK, S], F32, name=f"picked{a}") for a in range(PASSES)]
         grouped = [held.tile([P, S * PACK], BF16, align_bytes=64, name=f"grouped{a}") for a in range(PASSES)]
         codes = [held.tile([P, S], U32, align_bytes=64, name=f"codes{a}") for a in range(PASSES)]
         planes = [held.tile([P, S], U8, align_bytes=64, name=f"planes{a}") for a in range(PASSES)]

@@ -165,16 +165,20 @@ def tile_picked_sub_lin_none_sub_e_kernel(
         def add(dst, left, right, vs):
             nc.vector.tensor_tensor(out=dst[:, vs], in0=left[:, vs], in1=right[:, vs], op=ADD)
 
-        for vs in halves:
-            for d in range(1, D):
-                nc.scalar.activation(out=fetched[d - 1][:, vs], in_=neighbours(d, vs), func=COPY)
-        nc.vector.tensor_tensor(out=terms[0][:], in0=neighbours(0, slice(0, V)), in1=gates[:, 0, :], op=MULT)
-        scale(1, halves[0])
-        scale(2, halves[0])
-        add(first, terms[0], terms[1], halves[0])
-        scale(1, halves[1])
-        scale(2, halves[1])
-        add(first, terms[0], terms[1], halves[1])
-        for queue, vs in zip((nc.scalar, nc.sync), halves):
-            add(total, first, terms[2], vs)
-            queue.dma_start(out=out[:, vs], in_=total[:, vs])
+        def fetch(d, vs):
+            nc.vector.tensor_tensor(out=terms[d][:, vs], in0=neighbours(d, vs), in1=gates[:, d, vs], op=MULT)
+
+        low, high = halves
+        for d, vs in ((2, low), (1, high), (2, high)):
+            nc.scalar.activation(out=fetched[d - 1][:, vs], in_=neighbours(d, vs), func=COPY)
+        fetch(0, slice(0, V))
+        fetch(1, low)
+        scale(2, low)
+        scale(1, high)
+        add(first, terms[0], terms[2], low)
+        scale(2, high)
+        add(first, terms[0], terms[1], high)
+        add(total, first, terms[1], low)
+        nc.scalar.dma_start(out=out[:, low], in_=total[:, low])
+        add(total, first, terms[2], high)
+        nc.sync.dma_start(out=out[:, high], in_=total[:, high])

from contextlib import ExitStack

import concourse.mybir as mybir

K, T, D, S, V, N = 1536, 1024, 3, 512, 256, 128

F32 = mybir.dt.float32
BF16 = mybir.dt.bfloat16
I32 = mybir.dt.int32
U32 = mybir.dt.uint32
U16 = mybir.dt.uint16
U8 = mybir.dt.uint8
FP8X4 = mybir.dt.float8_e4m3fn_x4
ADD = mybir.AluOpType.add
MULT = mybir.AluOpType.mult
COPY = mybir.ActivationFunctionType.Copy

FLOPS = 2 * K * S * N + 5 * V * N

P = 128
PACK = 4
K_PASS = P * PACK
PASSES = K // K_PASS

VECTOR_SHARE = ((288, 288, 288, 256), (0, 192, 288, 256), (0, 128, 224, 224))
LAST_CUT = 384
LOADS = (((0, 2), (2, 4)), ((0, 2), (2, 3), (3, 4)), ((0, 1), (1, 2), (2, 3), (3, 4)))
PARTS = ((0, 256), (256, 384), (384, 512))


def tile_picked_sub_lin_none_sub_e_kernel(
    tc, xT, w_words, w_scales, gate, offs, pos1, pos2, pos3, out
):
    nc = tc.nc
    with ExitStack() as ctx:
        held = ctx.enter_context(tc.tile_pool(name="held", bufs=1))
        psum = ctx.enter_context(tc.psum_pool(name="psum", bufs=1))

        lists = [held.tile([P, src.shape[1]], U16, name=f"list{i}") for i, src in enumerate((offs, pos1, pos2, pos3))]
        w_codes = held.tile([P, PASSES, N], U32, align_bytes=64, name="w_codes")
        w_planes = held.tile([P, PASSES, N], U8, align_bytes=64, name="w_planes")
        gates = held.tile([P, D, V], F32, name="gates")

        nc.gpsimd.memset(w_planes[:].rearrange("p a m -> p (a m)").bitcast(I32), 0)

        warm = held.tile([P, 16], F32, name="warm")
        nc.vector.memset(warm[:, 0:1], 0.0)
        nc.scalar.activation(out=warm[:, 8:9], in_=warm[:, 0:1], func=COPY)
        raw = {}
        for a in range(PASSES):
            rows = xT[a * K_PASS : (a + 1) * K_PASS, :].rearrange("(p j) t -> p j t", j=PACK)
            for j0, j1 in LOADS[a]:
                tile = held.tile([P, j1 - j0, T], F32, name=f"raw_{a}_{j0}")
                nc.sync.dma_start(out=tile[:], in_=rows[:, j0:j1, :])
                for j in range(j0, j1):
                    raw[a, j] = tile[:, j - j0, :]
                if (a, j0) == (0, 0):
                    nc.sync.dma_start(out=lists[0][:], in_=offs)
        words = w_words.rearrange("a p m r -> p a (m r)").bitcast(I32)
        nc.sync.dma_start(out=w_codes[:, :1, :].bitcast(I32), in_=words[:, :1, :])
        for q in range(4):
            nc.sync.dma_start(
                out=w_planes[32 * q : 32 * q + 4, :, :].bitcast(I32),
                in_=w_scales[:, 4 * q : 4 * q + 4, :].rearrange("a q m -> q a m").bitcast(I32),
            )
        for a in range(1, PASSES):
            nc.sync.dma_start(out=w_codes[:, a, :].bitcast(I32), in_=words[:, a, :])
        nc.sync.dma_start(out=gates[:], in_=gate.rearrange("d m v -> m d v"))
        for tile, src in zip(lists[1:], (pos1, pos2, pos3)):
            nc.sync.dma_start(out=tile[:], in_=src)

        banks = [psum.tile([N, s1 - s0], F32, name=f"bank_{s0}") for s0, s1 in PARTS]
        y = held.tile([N, S], F32, name="y")
        picked = [held.tile([P, PACK, S], F32, name=f"picked{a}") for a in range(PASSES)]
        grouped = [held.tile([P, S * PACK], BF16, align_bytes=64, name=f"grouped{a}") for a in range(PASSES)]
        codes = [held.tile([P, S], U32, align_bytes=64, name=f"codes{a}") for a in range(PASSES)]
        planes = [held.tile([P, S], U8, align_bytes=64, name=f"planes{a}") for a in range(PASSES)]

        def pick(engine, a, j, s0, s1):
            window = raw[a, j].indirect(lists[0][:, s0 // 16 : s1 // 16])
            if engine == "scalar":
                nc.scalar.activation(out=picked[a][:, j, s0:s1], in_=window, func=COPY)
            else:
                nc.vector.tensor_copy(out=picked[a][:, j, s0:s1], in_=window)

        def pick_in_place(a, j, s0, s1):
            dst = grouped[a][:, PACK * s0 : PACK * s1].rearrange("p (s j) -> p s j", j=PACK)[:, :, j]
            nc.vector.tensor_copy(out=dst, in_=raw[a, j].indirect(lists[0][:, s0 // 16 : s1 // 16]))

        def place(a, j0, j1, s0, s1):
            dst = grouped[a][:, PACK * s0 : PACK * s1].rearrange("p (s j) -> p s j", j=PACK)[:, :, j0:j1]
            nc.vector.tensor_copy(out=dst, in_=picked[a][:, j0:j1, s0:s1].rearrange("p j s -> p s j"))

        def weave(a, s0, s1):
            dst = grouped[a][:, PACK * s0 : PACK * s1].rearrange("p (c i j) -> p c j i", i=4, j=PACK)
            nc.vector.tensor_copy(out=dst, in_=picked[a][:, :, s0:s1].rearrange("p j (c i) -> p c j i", i=4))

        def quantise(a, s0, s1):
            nc.vector.quantize_mx(
                out=codes[a][:, s0:s1].bitcast(FP8X4),
                scales=planes[a][:, s0:s1],
                in_=grouped[a][:, PACK * s0 : PACK * s1],
            )

        def product(a, part):
            s0, s1 = PARTS[part]
            nc.tensor.matmul_mx(
                out=banks[part][:],
                lhsT=w_codes[:, a, :].bitcast(FP8X4),
                lhsT_scale=w_planes[:, a, :],
                rhs=codes[a][:, s0:s1].bitcast(FP8X4),
                rhs_scale=planes[a][:, s0:s1],
                start=(a == 0),
                stop=(a == PASSES - 1),
            )

        last = PASSES - 1
        half = S // 2
        in_place = VECTOR_SHARE[last][-1]
        for a in range(PASSES):
            for j in range(PACK):
                share = VECTOR_SHARE[a][j]
                if a == last and j >= 2:
                    pick_in_place(a, j, 0, share)
                elif share:
                    pick("vector", a, j, 0, share)
                if (a, j) == (last, 1):
                    pick("scalar", a, j, share, in_place)
                    pick("scalar", a, j, in_place, S)
                    place(a, 0, 2, 0, in_place)
                elif (a, j) == (last, PACK - 1):
                    pick("scalar", a, j, share, LAST_CUT)
                    pick("scalar", a, j, LAST_CUT, S)
                else:
                    pick("scalar", a, j, share, S)
            if a < last:
                weave(a, 0, half)
                weave(a, half, S)
            else:
                weave(a, in_place, LAST_CUT)
                weave(a, LAST_CUT, S)
            for s0, s1 in PARTS if a == last else ((0, half), (half, S)):
                quantise(a, s0, s1)

        for a in range(PASSES):
            for part in range(len(PARTS)):
                product(a, part)

        nc.scalar.copy(out=y[:, slice(*PARTS[0])], in_=banks[0][:])
        nc.scalar.copy(out=y[:, slice(*PARTS[1])], in_=banks[1][:])
        nc.vector.tensor_copy(out=y[:, slice(*PARTS[2])], in_=banks[2][:])

        terms = [held.tile([N, V], F32, name=f"term{d}") for d in range(D)]
        fetched = [held.tile([N, V], F32, name=f"fetched{d}") for d in range(1, D)]
        first = held.tile([N, V], F32, name="first")
        total = held.tile([N, V], F32, name="total")
        halves = (slice(0, V // 2), slice(V // 2, V))

        def neighbours(d, vs):
            return y[:].indirect(lists[1 + d][:, vs.start // 16 : vs.stop // 16])

        def scale(d, vs):
            nc.vector.tensor_tensor(out=terms[d][:, vs], in0=fetched[d - 1][:, vs], in1=gates[:, d, vs], op=MULT)

        def add(dst, left, right, vs):
            nc.vector.tensor_tensor(out=dst[:, vs], in0=left[:, vs], in1=right[:, vs], op=ADD)

        def fetch(d, vs):
            nc.vector.tensor_tensor(out=terms[d][:, vs], in0=neighbours(d, vs), in1=gates[:, d, vs], op=MULT)

        low, high = halves
        for d, vs in ((2, low), (1, high), (2, high)):
            nc.scalar.activation(out=fetched[d - 1][:, vs], in_=neighbours(d, vs), func=COPY)
        fetch(0, slice(0, V))
        fetch(1, low)
        scale(2, low)
        scale(1, high)
        add(first, terms[0], terms[2], low)
        scale(2, high)
        add(first, terms[0], terms[1], high)
        add(total, first, terms[1], low)
        nc.scalar.dma_start(out=out[:, low], in_=total[:, low])
        add(total, first, terms[2], high)
        nc.sync.dma_start(out=out[:, high], in_=total[:, high])
